import numpy as np, ml_dtypes
CORES = [3,5,19,21,35,37,51,53,67,69]
N = 10
import mx_ref
NC, HD, G = 512, 1, 4
C, DEC = np.float32(0.047), np.float32(0.8)
BF = ml_dtypes.bfloat16
def cut(t, i, w=512):
    return t[:, w * i:w * i + w]
def tile(rs):
    return np.stack(rs, axis=2).reshape(128, -1).astype(BF)
def layer(w, X):
    out = []
    for i in range(G):
        for t in range(len(X)):
            p = mx_ref.matmul(mx_ref.quantize(cut(w, len(X) * i + t)), X[t])
            z = p if t == 0 else z + p
        out.append(z)
    return out
def pick(b):
    s = np.zeros((128, 128, 4), np.float32)
    s[np.arange(128), np.arange(128), b] = 1.0
    return mx_ref.quantize(s.reshape(128, 512).astype(BF))
def setup_inputs(rng):
    def f(*shape):
        return mx_ref.flush((rng.standard_normal(shape, dtype=np.float32) * np.exp2(rng.integers(-2, 3, shape[:-1] + (1,)))).astype(BF))
    return {"k": f(N, 128, HD * 4 * 512), "v": f(N, 128, HD * 512), "q": f(N, 128, HD * 4 * NC)}
def setup_inputs_blocks(rng):
    d = setup_inputs(rng)
    for k in ("k", "v", "q"): d[k] = mx_ref.spread(d[k], rng, 4)
    return d
def setup_inputs_wide(rng):
    d = setup_inputs(rng)
    for k in ("k", "v", "q"): d[k] = mx_ref.flush((d[k].astype(np.float32) * np.exp2(rng.integers(-4, 5, (N, 1, 1))).astype(np.float32)).astype(BF))
    return d
def setup_inputs_zeros(rng):
    d = setup_inputs(rng); v = d["v"].reshape(N, 128, -1, 4).copy()
    v[np.broadcast_to((rng.random((N, 1, v.shape[2], 1)) < 0.33), v.shape)] = 0
    d["v"] = v.reshape(d["v"].shape)
    return d
def reference(k, v, q):
    S = [pick(t) for t in range(4)]
    y = np.zeros((N, 128, HD * NC), np.float32)
    for a in range(HD):
        for r in range(N):
            R = [z * C for z in layer(cut(k[r], a, 4 * 512), [mx_ref.quantize(cut(v[r], a))])]
            if r > 0: R = [R[t] + mx_ref.matmul(S[t], s) * DEC for t in range(4)]
            s = mx_ref.quantize(tile(R))
            y[r][:, NC * a:NC * a + NC] = mx_ref.matmul(s, mx_ref.quantize(cut(q[r], a, 4 * NC)))
    return {"y": y}

@@ -1,0 +1,136 @@
+import numpy as np
+from concourse.mybir import dt, AluOpType, ActivationFunctionType
+
+ENG_ON = 4
+ENG_OFF = 4
+C = float(np.float32(0.047))
+DEC = float(np.float32(0.8))
+BF, F32, U8, X4 = "bfloat16", "float32", "uint8", "float8_e4m3fn_x4"
+
+SCRATCH = {
+    "kt": ("sbuf", [128, 2048], BF), "vt": ("sbuf", [128, 512], BF), "qt": ("sbuf", [128, 2048], BF),
+    "kc": ("sbuf", [128, 512], X4), "ks": ("sbuf", [128, 512], U8),
+    "vc": ("sbuf", [128, 128], X4), "vs": ("sbuf", [128, 128], U8),
+    "qc": ("sbuf", [128, 512], X4), "qs": ("sbuf", [128, 512], U8),
+    "ones": ("sbuf", [128, 516], BF), "w": ("sbuf", [128, 516], BF),
+    "pc": ("sbuf", [128, 512], X4), "ps": ("sbuf", [128, 512], U8),
+    "zc": ("sbuf", [128, 512], F32),
+    "e": ("sbuf", [128, 512], F32),
+    "tl": ("sbuf", [128, 512], BF),
+    "sc": ("sbuf", [128, 128], X4), "ss": ("sbuf", [128, 128], U8),
+    "lc": ("sbuf", [128, 128], X4), "ls": ("sbuf", [128, 128], U8),
+    "yt": ("sbuf", [128, 512], F32),
+    "pz": ("psum", [128, 2048], F32), "pd": ("psum", [128, 2048], F32),
+}
+SEMAPHORES = ["ldv", "lda", "ldb", "ldq", "one", "wsel", "pq", "qv", "ka", "kb", "qq", "zc", "tile", "state",
+              "arr", "sent", "y0", "y1", "c0", "c1", "st0", "st1",
+              "z0", "z1", "z2", "z3", "d0", "d1", "d2", "d3", "e0", "e1", "e2", "e3"]
+
+
+def engines(topo, src, dst, n):
+    m = topo.mask(src, dst)
+    bits = [1 << i for i in range(m.bit_length()) if (m >> i) & 1]
+    return sum(bits[::len(bits) // n])
+
+
+def rank_program(g, core, T, topo):
+    rank = T.rank_of(core)
+    if rank is None:
+        return
+    last = len(T.cores) - 1
+    S, V, P, A = T.sem, g.vector, g.tensor, g.scalar
+    MULT, COPY = AluOpType.mult, ActivationFunctionType.Copy
+    blk = lambda t, b, n=128: t[:, n * b:n * (b + 1)]
+    pz = lambda b, n=128: T.pz[:, 512 * b:512 * b + n]
+    pd = lambda b: T.pd[:, 512 * b:512 * b + 128]
+    tcol = lambda b: T.tl[:, b:512:4]
+    q_early = rank > 1
+
+    g.sync.dma_start(T.vt[:], T.v[:]).then_inc(S.ldv, 16)
+    A.dma_start(T.kt[:, 0:1024], T.k[:, 0:1024]).then_inc(S.lda, 16)
+    g.sync.dma_start(T.kt[:, 1024:2048], T.k[:, 1024:2048]).then_inc(S.ldb, 16)
+    g.sync.wait_ge(S.lda, 16)
+    g.sync.wait_ge(S.ldb, 16)
+    g.sync.dma_start(T.qt[:], T.q[:]).then_inc(S.ldq, 16)
+
+    if rank > 0:
+        V.memset(T.ones[:], 1.0).then_inc(S.one, 1)
+        g.wait_ge(S.one, 1)
+        g.affine_select(T.w[:], T.ones[:], [[1, 516]], AluOpType.is_equal, 0.0, -3, -4).then_inc(S.wsel, 1)
+        V.wait_ge(S.wsel, 1)
+        for b in range(4):
+            V.quantize_mx(blk(T.pc, b), blk(T.ps, b), T.w[:, 3 - b:515 - b]).then_inc(S.pq, 1)
+    V.wait_ge(S.ldv, 16)
+    V.quantize_mx(T.vc[:], T.vs[:], T.vt[:]).then_inc(S.qv, 1)
+    V.wait_ge(S.lda, 16)
+    V.quantize_mx(T.kc[:, 0:256], T.ks[:, 0:256], T.kt[:, 0:1024]).then_inc(S.ka, 1)
+    V.wait_ge(S.ldb, 16)
+    V.quantize_mx(T.kc[:, 256:512], T.ks[:, 256:512], T.kt[:, 1024:2048]).then_inc(S.kb, 1)
+
+    P.wait_ge(S.qv, 1)
+    for b in range(4):
+        if b == 0:
+            P.wait_ge(S.ka, 1)
+        if b == 2:
+            P.wait_ge(S.kb, 1)
+        P.matmul_mx(pz(b), blk(T.kc, b), blk(T.ks, b), T.vc[:], T.vs[:], True, True).then_inc(S["z%d" % b], 1)
+
+    if rank == 0:
+        for b in range(3):
+            A.wait_ge(S["z%d" % b], 1)
+            A.activation(tcol(b), pz(b), COPY, scale=C).then_inc(S.tile, 1)
+        V.wait_ge(S.z3, 1)
+        V.tensor_scalar(tcol(3), pz(3), C, None, MULT).then_inc(S.tile, 1)
+    else:
+        for b in range(4):
+            A.wait_ge(S["z%d" % b], 1)
+            A.activation(blk(T.zc, b), pz(b), COPY, scale=C).then_inc(S.zc, 1)
+        V.wait_ge(S.zc, 4)
+        if q_early:
+            V.wait_ge(S.ldq, 16)
+            V.quantize_mx(T.qc[:], T.qs[:], T.qt[:]).then_inc(S.qq, 1)
+        n = ENG_ON if topo.chip(T.cores[rank - 1]) == topo.chip(core) else ENG_OFF
+        P.wait_ge(S.pq, 4)
+        P.wait_ge(S.arr, 2 * n)
+        for b in range(4):
+            P.matmul_mx(pd(b), blk(T.pc, b), blk(T.ps, b), T.lc[:], T.ls[:], True, True).then_inc(S["d%d" % b], 1)
+        V.wait_ge(S.d0, 1)
+        V.tensor_scalar(blk(T.e, 0), pd(0), DEC, None, MULT).then_inc(S.e0, 1)
+        for b in range(1, 4):
+            A.wait_ge(S["d%d" % b], 1)
+            A.activation(blk(T.e, b), pd(b), COPY, scale=DEC).then_inc(S["e%d" % b], 1)
+        for b in range(4):
+            V.wait_ge(S["e%d" % b], 1)
+            V.tensor_tensor(tcol(b), blk(T.e, b), blk(T.zc, b), AluOpType.add).then_inc(S.tile, 1)
+    V.wait_ge(S.tile, 4)
+    V.quantize_mx(T.sc[:], T.ss[:], T.tl[:]).then_inc(S.state, 1)
+    if not q_early:
+        V.wait_ge(S.ldq, 16)
+        V.quantize_mx(T.qc[:], T.qs[:], T.qt[:]).then_inc(S.qq, 1)
+
+    if rank < last:
+        nxt = T.cores[rank + 1]
+        rid, pid = topo.addr(nxt)[:2]
+        n = ENG_ON if topo.chip(nxt) == topo.chip(core) else ENG_OFF
+        m = engines(topo, core, nxt, n)
+        g.wait_ge(S.state, 1)
+        g.remote_dma(T.lc[:].bitcast(dt.uint8), T.sc[:].bitcast(dt.uint8), S.arr, S.sent, pid, rid, m)
+        g.remote_dma(T.ls[:], T.ss[:], S.arr, S.sent, pid, rid, m)
+        g.wait_ge(S.sent, 2 * n)
+        g.sync.wait_ge(S.sent, 2 * n)
+        A.wait_ge(S.sent, 2 * n)
+
+    P.wait_ge(S.qq, 1)
+    P.wait_ge(S.state, 1)
+    for h in range(2):
+        P.matmul_mx(pz(h, 256), T.sc[:], T.ss[:], blk(T.qc, h, 256), blk(T.qs, h, 256), True, True).then_inc(S["y%d" % h], 1)
+    V.wait_ge(S.y0, 1)
+    V.tensor_copy(blk(T.yt, 0, 256), pz(0, 256)).then_inc(S.c0, 1)
+    g.sync.wait_ge(S.c0, 1)
+    g.sync.dma_start(T.y[:, 0:256], blk(T.yt, 0, 256)).then_inc(S.st0, 16)
+    A.wait_ge(S.y1, 1)
+    A.activation(blk(T.yt, 1, 256), pz(1, 256), COPY).then_inc(S.c1, 1)
+    A.wait_ge(S.c1, 1)
+    A.dma_start(T.y[:, 256:512], blk(T.yt, 1, 256)).then_inc(S.st1, 16)
+    g.sync.wait_ge(S.st0, 16)
+    A.wait_ge(S.st1, 16)

@@ -1,8 +1,7 @@
 import numpy as np
 from concourse.mybir import dt, AluOpType, ActivationFunctionType
 
-ENG_ON = 4
-ENG_OFF = 4
+ENG_ON, ENG_OFF = 8, 4
 C = float(np.float32(0.047))
 DEC = float(np.float32(0.8))
 BF, F32, U8, X4 = "bfloat16", "float32", "uint8", "float8_e4m3fn_x4"
@@ -22,9 +21,9 @@ SCRATCH = {
     "yt": ("sbuf", [128, 512], F32),
     "pz": ("psum", [128, 2048], F32), "pd": ("psum", [128, 2048], F32),
 }
-SEMAPHORES = ["ldv", "lda", "ldb", "ldq", "one", "wsel", "pq", "qv", "ka", "kb", "qq", "zc", "tile", "state",
-              "arr", "sent", "y0", "y1", "c0", "c1", "st0", "st1",
-              "z0", "z1", "z2", "z3", "d0", "d1", "d2", "d3", "e0", "e1", "e2", "e3"]
+SEMAPHORES = ["ldv", "lda", "ldb", "ldq", "one", "wsel", "pq", "qv", "k0", "k1", "k2", "k3", "qq", "zc", "tile", "state",
+              "arr", "sent", "y0", "y1", "y2", "y3", "c0", "c1", "st0", "st1",
+              "z0", "z1", "z2", "z3", "d0", "d1", "d2", "d3", "e0a", "e0b", "e1", "e2", "e3"]
 
 
 def engines(topo, src, dst, n):
@@ -39,16 +38,17 @@ def rank_program(g, core, T, topo):
         return
     last = len(T.cores) - 1
     S, V, P, A = T.sem, g.vector, g.tensor, g.scalar
-    MULT, COPY = AluOpType.mult, ActivationFunctionType.Copy
+    MULT, ADD, COPY = AluOpType.mult, AluOpType.add, ActivationFunctionType.Copy
     blk = lambda t, b, n=128: t[:, n * b:n * (b + 1)]
-    pz = lambda b, n=128: T.pz[:, 512 * b:512 * b + n]
+    pz = lambda b: T.pz[:, 512 * b:512 * b + 128]
     pd = lambda b: T.pd[:, 512 * b:512 * b + 128]
     tcol = lambda b: T.tl[:, b:512:4]
+    count = lambda a, b: ENG_ON if topo.chip(a) == topo.chip(b) else ENG_OFF
     q_early = rank > 1
 
     g.sync.dma_start(T.vt[:], T.v[:]).then_inc(S.ldv, 16)
-    A.dma_start(T.kt[:, 0:1024], T.k[:, 0:1024]).then_inc(S.lda, 16)
-    g.sync.dma_start(T.kt[:, 1024:2048], T.k[:, 1024:2048]).then_inc(S.ldb, 16)
+    A.dma_start(T.kt[:, 0:1536], T.k[:, 0:1536]).then_inc(S.lda, 16)
+    g.sync.dma_start(T.kt[:, 1536:2048], T.k[:, 1536:2048]).then_inc(S.ldb, 16)
     g.sync.wait_ge(S.lda, 16)
     g.sync.wait_ge(S.ldb, 16)
     g.sync.dma_start(T.qt[:], T.q[:]).then_inc(S.ldq, 16)
@@ -62,17 +62,16 @@ def rank_program(g, core, T, topo):
             V.quantize_mx(blk(T.pc, b), blk(T.ps, b), T.w[:, 3 - b:515 - b]).then_inc(S.pq, 1)
     V.wait_ge(S.ldv, 16)
     V.quantize_mx(T.vc[:], T.vs[:], T.vt[:]).then_inc(S.qv, 1)
-    V.wait_ge(S.lda, 16)
-    V.quantize_mx(T.kc[:, 0:256], T.ks[:, 0:256], T.kt[:, 0:1024]).then_inc(S.ka, 1)
-    V.wait_ge(S.ldb, 16)
-    V.quantize_mx(T.kc[:, 256:512], T.ks[:, 256:512], T.kt[:, 1024:2048]).then_inc(S.kb, 1)
+    for b in range(4):
+        if b == 0:
+            V.wait_ge(S.lda, 16)
+        if b == 3:
+            V.wait_ge(S.ldb, 16)
+        V.quantize_mx(blk(T.kc, b), blk(T.ks, b), blk(T.kt, b, 512)).then_inc(S["k%d" % b], 1)
 
     P.wait_ge(S.qv, 1)
     for b in range(4):
-        if b == 0:
-            P.wait_ge(S.ka, 1)
-        if b == 2:
-            P.wait_ge(S.kb, 1)
+        P.wait_ge(S["k%d" % b], 1)
         P.matmul_mx(pz(b), blk(T.kc, b), blk(T.ks, b), T.vc[:], T.vs[:], True, True).then_inc(S["z%d" % b], 1)
 
     if rank == 0:
@@ -81,6 +80,7 @@ def rank_program(g, core, T, topo):
             A.activation(tcol(b), pz(b), COPY, scale=C).then_inc(S.tile, 1)
         V.wait_ge(S.z3, 1)
         V.tensor_scalar(tcol(3), pz(3), C, None, MULT).then_inc(S.tile, 1)
+        V.wait_ge(S.tile, 4)
     else:
         for b in range(4):
             A.wait_ge(S["z%d" % b], 1)
@@ -89,20 +89,24 @@ def rank_program(g, core, T, topo):
         if q_early:
             V.wait_ge(S.ldq, 16)
             V.quantize_mx(T.qc[:], T.qs[:], T.qt[:]).then_inc(S.qq, 1)
-        n = ENG_ON if topo.chip(T.cores[rank - 1]) == topo.chip(core) else ENG_OFF
         P.wait_ge(S.pq, 4)
-        P.wait_ge(S.arr, 2 * n)
+        P.wait_ge(S.arr, 2 * count(T.cores[rank - 1], core))
         for b in range(4):
             P.matmul_mx(pd(b), blk(T.pc, b), blk(T.ps, b), T.lc[:], T.ls[:], True, True).then_inc(S["d%d" % b], 1)
-        V.wait_ge(S.d0, 1)
-        V.tensor_scalar(blk(T.e, 0), pd(0), DEC, None, MULT).then_inc(S.e0, 1)
         for b in range(1, 4):
             A.wait_ge(S["d%d" % b], 1)
             A.activation(blk(T.e, b), pd(b), COPY, scale=DEC).then_inc(S["e%d" % b], 1)
-        for b in range(4):
+        V.wait_ge(S.d0, 1)
+        V.tensor_scalar(T.e[:, 0:64], T.pd[:, 0:64], DEC, None, MULT).then_inc(S.e0a, 1)
+        V.tensor_scalar(T.e[:, 64:128], T.pd[:, 64:128], DEC, None, MULT).then_inc(S.e0b, 1)
+        V.wait_ge(S.e0a, 1)
+        V.tensor_tensor(T.tl[:, 0:256:4], T.e[:, 0:64], T.zc[:, 0:64], ADD).then_inc(S.tile, 1)
+        V.wait_ge(S.e0b, 1)
+        V.tensor_tensor(T.tl[:, 256:512:4], T.e[:, 64:128], T.zc[:, 64:128], ADD).then_inc(S.tile, 1)
+        for b in range(1, 4):
             V.wait_ge(S["e%d" % b], 1)
-            V.tensor_tensor(tcol(b), blk(T.e, b), blk(T.zc, b), AluOpType.add).then_inc(S.tile, 1)
-    V.wait_ge(S.tile, 4)
+            V.tensor_tensor(tcol(b), blk(T.e, b), blk(T.zc, b), ADD).then_inc(S.tile, 1)
+        V.wait_ge(S.tile, 5)
     V.quantize_mx(T.sc[:], T.ss[:], T.tl[:]).then_inc(S.state, 1)
     if not q_early:
         V.wait_ge(S.ldq, 16)
@@ -111,7 +115,7 @@ def rank_program(g, core, T, topo):
     if rank < last:
         nxt = T.cores[rank + 1]
         rid, pid = topo.addr(nxt)[:2]
-        n = ENG_ON if topo.chip(nxt) == topo.chip(core) else ENG_OFF
+        n = count(core, nxt)
         m = engines(topo, core, nxt, n)
         g.wait_ge(S.state, 1)
         g.remote_dma(T.lc[:].bitcast(dt.uint8), T.sc[:].bitcast(dt.uint8), S.arr, S.sent, pid, rid, m)
@@ -122,15 +126,17 @@ def rank_program(g, core, T, topo):
 
     P.wait_ge(S.qq, 1)
     P.wait_ge(S.state, 1)
-    for h in range(2):
-        P.matmul_mx(pz(h, 256), T.sc[:], T.ss[:], blk(T.qc, h, 256), blk(T.qs, h, 256), True, True).then_inc(S["y%d" % h], 1)
-    V.wait_ge(S.y0, 1)
-    V.tensor_copy(blk(T.yt, 0, 256), pz(0, 256)).then_inc(S.c0, 1)
-    g.sync.wait_ge(S.c0, 1)
+    for h in range(4):
+        P.matmul_mx(pz(h), T.sc[:], T.ss[:], blk(T.qc, h), blk(T.qs, h), True, True).then_inc(S["y%d" % h], 1)
+    for h in (0, 2):
+        V.wait_ge(S["y%d" % h], 1)
+        V.tensor_copy(blk(T.yt, h), pz(h)).then_inc(S["c%d" % (h // 2)], 1)
+    for h in (1, 3):
+        A.wait_ge(S["y%d" % h], 1)
+        A.activation(blk(T.yt, h), pz(h), COPY).then_inc(S["c%d" % (h // 2)], 1)
+    g.sync.wait_ge(S.c0, 2)
     g.sync.dma_start(T.y[:, 0:256], blk(T.yt, 0, 256)).then_inc(S.st0, 16)
-    A.wait_ge(S.y1, 1)
-    A.activation(blk(T.yt, 1, 256), pz(1, 256), COPY).then_inc(S.c1, 1)
-    A.wait_ge(S.c1, 1)
+    A.wait_ge(S.c1, 2)
     A.dma_start(T.y[:, 256:512], blk(T.yt, 1, 256)).then_inc(S.st1, 16)
     g.sync.wait_ge(S.st0, 16)
     A.wait_ge(S.st1, 16)

import numpy as np
from concourse.mybir import dt, AluOpType, ActivationFunctionType

ENG_ON, ENG_OFF = 8, 4
C = float(np.float32(0.047))
DEC = float(np.float32(0.8))
BF, F32, U8, X4 = "bfloat16", "float32", "uint8", "float8_e4m3fn_x4"

SCRATCH = {
    "kt": ("sbuf", [128, 2048], BF), "vt": ("sbuf", [128, 512], BF), "qt": ("sbuf", [128, 2048], BF),
    "kc": ("sbuf", [128, 512], X4), "ks": ("sbuf", [128, 512], U8),
    "vc": ("sbuf", [128, 128], X4), "vs": ("sbuf", [128, 128], U8),
    "qc": ("sbuf", [128, 512], X4), "qs": ("sbuf", [128, 512], U8),
    "ones": ("sbuf", [128, 516], BF), "w": ("sbuf", [128, 516], BF),
    "pc": ("sbuf", [128, 512], X4), "ps": ("sbuf", [128, 512], U8),
    "zc": ("sbuf", [128, 512], F32),
    "e": ("sbuf", [128, 512], F32),
    "tl": ("sbuf", [128, 512], BF),
    "sc": ("sbuf", [128, 128], X4), "ss": ("sbuf", [128, 128], U8),
    "lc": ("sbuf", [128, 128], X4), "ls": ("sbuf", [128, 128], U8),
    "yt": ("sbuf", [128, 512], F32),
    "pz": ("psum", [128, 2048], F32), "pd": ("psum", [128, 2048], F32),
}
SEMAPHORES = ["ldv", "lda", "ldb", "ldq", "one", "wsel", "pq", "qv", "k0", "k1", "k2", "k3", "qq", "zc", "tile", "state",
              "arr", "sent", "y0", "y1", "y2", "y3", "c0", "c1", "st0", "st1",
              "z0", "z1", "z2", "z3", "d0", "d1", "d2", "d3", "e0a", "e0b", "e1", "e2", "e3"]


def engines(topo, src, dst, n):
    m = topo.mask(src, dst)
    bits = [1 << i for i in range(m.bit_length()) if (m >> i) & 1]
    return sum(bits[::len(bits) // n])


def rank_program(g, core, T, topo):
    rank = T.rank_of(core)
    if rank is None:
        return
    last = len(T.cores) - 1
    S, V, P, A = T.sem, g.vector, g.tensor, g.scalar
    MULT, ADD, COPY = AluOpType.mult, AluOpType.add, ActivationFunctionType.Copy
    blk = lambda t, b, n=128: t[:, n * b:n * (b + 1)]
    pz = lambda b: T.pz[:, 512 * b:512 * b + 128]
    pd = lambda b: T.pd[:, 512 * b:512 * b + 128]
    tcol = lambda b: T.tl[:, b:512:4]
    count = lambda a, b: ENG_ON if topo.chip(a) == topo.chip(b) else ENG_OFF
    q_early = rank > 1

    g.sync.dma_start(T.vt[:], T.v[:]).then_inc(S.ldv, 16)
    A.dma_start(T.kt[:, 0:1536], T.k[:, 0:1536]).then_inc(S.lda, 16)
    g.sync.dma_start(T.kt[:, 1536:2048], T.k[:, 1536:2048]).then_inc(S.ldb, 16)
    g.sync.wait_ge(S.lda, 16)
    g.sync.wait_ge(S.ldb, 16)
    g.sync.dma_start(T.qt[:], T.q[:]).then_inc(S.ldq, 16)

    if rank > 0:
        V.memset(T.ones[:], 1.0).then_inc(S.one, 1)
        g.wait_ge(S.one, 1)
        g.affine_select(T.w[:], T.ones[:], [[1, 516]], AluOpType.is_equal, 0.0, -3, -4).then_inc(S.wsel, 1)
        V.wait_ge(S.wsel, 1)
        for b in range(4):
            V.quantize_mx(blk(T.pc, b), blk(T.ps, b), T.w[:, 3 - b:515 - b]).then_inc(S.pq, 1)
    V.wait_ge(S.ldv, 16)
    V.quantize_mx(T.vc[:], T.vs[:], T.vt[:]).then_inc(S.qv, 1)
    for b in range(4):
        if b == 0:
            V.wait_ge(S.lda, 16)
        if b == 3:
            V.wait_ge(S.ldb, 16)
        V.quantize_mx(blk(T.kc, b), blk(T.ks, b), blk(T.kt, b, 512)).then_inc(S["k%d" % b], 1)

    P.wait_ge(S.qv, 1)
    for b in range(4):
        P.wait_ge(S["k%d" % b], 1)
        P.matmul_mx(pz(b), blk(T.kc, b), blk(T.ks, b), T.vc[:], T.vs[:], True, True).then_inc(S["z%d" % b], 1)

    if rank == 0:
        for b in range(3):
            A.wait_ge(S["z%d" % b], 1)
            A.activation(tcol(b), pz(b), COPY, scale=C).then_inc(S.tile, 1)
        V.wait_ge(S.z3, 1)
        V.tensor_scalar(tcol(3), pz(3), C, None, MULT).then_inc(S.tile, 1)
        V.wait_ge(S.tile, 4)
    else:
        for b in range(4):
            A.wait_ge(S["z%d" % b], 1)
            A.activation(blk(T.zc, b), pz(b), COPY, scale=C).then_inc(S.zc, 1)
        V.wait_ge(S.zc, 4)
        if q_early:
            V.wait_ge(S.ldq, 16)
            V.quantize_mx(T.qc[:], T.qs[:], T.qt[:]).then_inc(S.qq, 1)
        P.wait_ge(S.pq, 4)
        P.wait_ge(S.arr, 2 * count(T.cores[rank - 1], core))
        for b in range(4):
            P.matmul_mx(pd(b), blk(T.pc, b), blk(T.ps, b), T.lc[:], T.ls[:], True, True).then_inc(S["d%d" % b], 1)
        for b in range(1, 4):
            A.wait_ge(S["d%d" % b], 1)
            A.activation(blk(T.e, b), pd(b), COPY, scale=DEC).then_inc(S["e%d" % b], 1)
        V.wait_ge(S.d0, 1)
        V.tensor_scalar(T.e[:, 0:64], T.pd[:, 0:64], DEC, None, MULT).then_inc(S.e0a, 1)
        V.tensor_scalar(T.e[:, 64:128], T.pd[:, 64:128], DEC, None, MULT).then_inc(S.e0b, 1)
        V.wait_ge(S.e0a, 1)
        V.tensor_tensor(T.tl[:, 0:256:4], T.e[:, 0:64], T.zc[:, 0:64], ADD).then_inc(S.tile, 1)
        V.wait_ge(S.e0b, 1)
        V.tensor_tensor(T.tl[:, 256:512:4], T.e[:, 64:128], T.zc[:, 64:128], ADD).then_inc(S.tile, 1)
        for b in range(1, 4):
            V.wait_ge(S["e%d" % b], 1)
            V.tensor_tensor(tcol(b), blk(T.e, b), blk(T.zc, b), ADD).then_inc(S.tile, 1)
        V.wait_ge(S.tile, 5)
    V.quantize_mx(T.sc[:], T.ss[:], T.tl[:]).then_inc(S.state, 1)
    if not q_early:
        V.wait_ge(S.ldq, 16)
        V.quantize_mx(T.qc[:], T.qs[:], T.qt[:]).then_inc(S.qq, 1)

    if rank < last:
        nxt = T.cores[rank + 1]
        rid, pid = topo.addr(nxt)[:2]
        n = count(core, nxt)
        m = engines(topo, core, nxt, n)
        g.wait_ge(S.state, 1)
        g.remote_dma(T.lc[:].bitcast(dt.uint8), T.sc[:].bitcast(dt.uint8), S.arr, S.sent, pid, rid, m)
        g.remote_dma(T.ls[:], T.ss[:], S.arr, S.sent, pid, rid, m)
        g.wait_ge(S.sent, 2 * n)
        g.sync.wait_ge(S.sent, 2 * n)
        A.wait_ge(S.sent, 2 * n)

    P.wait_ge(S.qq, 1)
    P.wait_ge(S.state, 1)
    for h in range(4):
        P.matmul_mx(pz(h), T.sc[:], T.ss[:], blk(T.qc, h), blk(T.qs, h), True, True).then_inc(S["y%d" % h], 1)
    for h in (0, 2):
        V.wait_ge(S["y%d" % h], 1)
        V.tensor_copy(blk(T.yt, h), pz(h)).then_inc(S["c%d" % (h // 2)], 1)
    for h in (1, 3):
        A.wait_ge(S["y%d" % h], 1)
        A.activation(blk(T.yt, h), pz(h), COPY).then_inc(S["c%d" % (h // 2)], 1)
    g.sync.wait_ge(S.c0, 2)
    g.sync.dma_start(T.y[:, 0:256], blk(T.yt, 0, 256)).then_inc(S.st0, 16)
    A.wait_ge(S.c1, 2)
    A.dma_start(T.y[:, 256:512], blk(T.yt, 1, 256)).then_inc(S.st1, 16)
    g.sync.wait_ge(S.st0, 16)
    A.wait_ge(S.st1, 16)
